import numpy as np
import ml_dtypes


def mxq(x, axis, fmt="e4m3"):
    dtype, down = {"e4m3": (ml_dtypes.float8_e4m3fn, 7), "e5m2": (ml_dtypes.float8_e5m2, 14)}[fmt]
    v = np.moveaxis(np.asarray(x, np.float32).astype(ml_dtypes.bfloat16).astype(np.float64), axis, -1)
    blocks = v.reshape(v.shape[:-1] + (-1, 32))
    amax = np.abs(blocks).max(-1, keepdims=True)
    byte = np.maximum(np.where(amax > 0, np.frexp(amax)[1] - 1 + 127, 0) - down, 1)
    scale = np.exp2(byte - 127.0)
    codes = (blocks / scale).astype(np.float32).astype(dtype).astype(np.float64)
    return np.moveaxis((codes * scale).reshape(v.shape), -1, axis)


WIDE = False


def mx_kscale(k):
    if not WIDE:
        return np.ones(k)
    levels = np.array([10, -10, 5, -5, 0])
    if k % 512:
        return np.exp2(np.random.permutation(np.resize(levels, k // 32))).repeat(32)
    a = np.empty((k // 512, 16))
    for p in range(k // 512):
        a[p, :8] = np.random.permutation(np.resize(levels, 8))
        for g in range(8):
            far = levels[np.abs(levels - a[p, g]) >= 10]
            a[p, g + 8] = far[np.random.randint(len(far))]
    return np.exp2(a.ravel()).repeat(32)


def f64(x):
    return np.asarray(x).astype(np.float64)


def striped(idx):
    return np.tile(idx.reshape(-1, 16).T, (8, 1)).astype(np.uint16)


def unstriped(offs):
    return offs[:16].T.reshape(-1).astype(np.int64)


def striped8(idx):
    return np.concatenate([x.reshape(-1, 16).T for x in idx]).astype(np.uint16)


def runs(offs, k):
    lists = np.stack([offs[16 * r : 16 * r + 16].T.reshape(-1) for r in range(8)]).astype(np.int64)
    return lists[np.arange(k) % 512 // 64]


def pack_weight(w):
    k, n = w.shape
    w = f64(np.asarray(w, np.float32).astype(ml_dtypes.bfloat16)).reshape(k // 32, 32, n)
    amax = np.abs(w).max(1)
    byte = np.clip(np.where(amax > 0, np.frexp(amax)[1] - 1 + 127 - 7, 1), 1, 254)
    scaled = (w * np.exp2(127.0 - byte)[:, None, :]).reshape(k, n).astype(np.float32)
    words = np.ascontiguousarray(scaled.reshape(k // 512, 128, 4, n).transpose(0, 1, 3, 2)).astype(ml_dtypes.float8_e4m3fn).view(np.uint8)
    return words, np.ascontiguousarray(byte.astype(np.uint8).reshape(k // 512, 16, n))


def unpack_weight(words, scales):
    g, p, n, _ = words.shape
    vals = np.ascontiguousarray(words).view(ml_dtypes.float8_e4m3fn).astype(np.float64) * np.repeat(np.exp2(scales.astype(np.float64) - 127.0), 8, axis=1)[..., None]
    return vals.transpose(0, 1, 3, 2).reshape(g * 512, n)


K, T, S, H, C, W = 512, 2048, 256, 512, 512, 1024


def setup_inputs():
    n = np.random.standard_normal
    s = mx_kscale(K)[:, None]
    packed_xT = pack_weight(n((K, T)) * s)
    return {
        "x_words": packed_xT[0],
        "x_scales": packed_xT[1],
        "w1": (n((K, H)) / np.sqrt(K) / s).astype(np.float32),
        "gs": (np.random.uniform(0.5, 1.5, (K, 1)) / s).astype(np.float32),
        "offs": striped(np.random.permutation(T)[:S]),
        "n1": striped8(np.stack([np.random.permutation(S) for _ in range(8)])),
        "n2": striped8(np.stack([np.random.permutation(S) for _ in range(8)])),
        "cand": striped(np.random.permutation(T)[:C]),
        "n3": striped(np.random.randint(0, S, W)),
    }


def reference(x_words, x_scales, w1, gs, offs, n1, n2, cand, n3):
    x_cand = unpack_weight(x_words, x_scales)[:, unstriped(cand)]
    xq = unpack_weight(x_words, x_scales)[:, unstriped(offs)]
    y = mxq(f64(w1), 0, "e4m3").T @ xq
    z = f64(gs) * (y - (np.minimum(y[np.arange(H)[:, None], runs(n1, H)], y[np.arange(H)[:, None], runs(n2, H)])))
    s = 0.0625 * ((x_cand.T @ mxq(z, 0, "e4m3")))
    mb = s[:, unstriped(n3)]
    mx = mb.reshape(C, S, 4).max(axis=2)
    mn = mb.reshape(C, S, 4).min(axis=2)
    return mx - (0.5 * mn)

@@ -1,0 +1,174 @@
+from contextlib import ExitStack
+
+import concourse.mybir as mybir
+
+K, T, S, H, C, W = 512, 2048, 256, 512, 512, 1024
+FLOPS = 2 * K * H * S + 2 * K * C * S
+
+F32 = mybir.dt.float32
+BF16 = mybir.dt.bfloat16
+I32 = mybir.dt.int32
+U32 = mybir.dt.uint32
+U16 = mybir.dt.uint16
+U8 = mybir.dt.uint8
+FP8X4 = mybir.dt.float8_e4m3fn_x4
+ALU = mybir.AluOpType
+COPY = mybir.ActivationFunctionType.Copy
+
+P = 128
+PACK = 4
+LANES = 16
+MEMBERS = 4
+HALF = S // 2
+S_WINDOW = 528
+M_SPLIT = 64
+
+
+def tile_picked_candundergspan_none_p_kernel(tc, x_words, x_scales, w1, gs, offs, n1, n2, cand, n3, out):
+    nc = tc.nc
+    with ExitStack() as ctx:
+        keep = ctx.enter_context(tc.tile_pool(name="keep", bufs=1))
+        ring = ctx.enter_context(tc.tile_pool(name="ring", bufs=3))
+        psum = ctx.enter_context(tc.psum_pool(name="psum", bufs=1))
+
+        offs_sb = keep.tile([P, S // LANES], U16, name="offs_sb")
+        cand_sb = keep.tile([P, C // LANES], U16, name="cand_sb")
+        n1_sb = keep.tile([P, S // LANES], U16, name="n1_sb")
+        n2_sb = keep.tile([P, S // LANES], U16, name="n2_sb")
+        n3_sb = keep.tile([P, W // LANES], U16, name="n3_sb")
+        w_raw = keep.tile([P, PACK, H], F32, name="w_raw")
+        words = keep.tile([P, T], U32, name="words", align_bytes=64)
+        scales = keep.tile([P, T], U8, name="scales", align_bytes=64)
+        gain = keep.tile([P, PACK], F32, name="gain")
+
+        nc.vector.memset(scales[:].bitcast(I32), 0)
+        nc.sync.dma_start(offs_sb[:], offs)
+        nc.sync.dma_start(cand_sb[:], cand)
+        nc.sync.dma_start(w_raw[:], w1.rearrange("(p j) c -> p j c", j=PACK))
+        nc.sync.dma_start(words[:].bitcast(I32), x_words[0].rearrange("p n r -> p (n r)").bitcast(I32))
+        for q in range(4):
+            nc.scalar.dma_start(scales[32 * q : 32 * q + 4, :].bitcast(I32), x_scales[0][4 * q : 4 * q + 4, :].bitcast(I32))
+        nc.sync.dma_start(n1_sb[:], n1)
+        nc.sync.dma_start(n2_sb[:], n2)
+        nc.sync.dma_start(gain[:], gs.rearrange("(p t) o -> p (t o)", t=PACK))
+        nc.sync.dma_start(n3_sb[:], n3)
+
+        s_rows = [keep.tile([P, S_WINDOW], F32, name=f"s_rows{c}") for c in range(C // P)]
+        for c in range(C // P):
+            nc.gpsimd.memset(s_rows[c][:, S:], 0.0)
+
+        xq_words = keep.tile([P, S], U32, name="xq_words", align_bytes=64)
+        xq_scales = keep.tile([P, S], U8, name="xq_scales", align_bytes=64)
+        xc_words = keep.tile([P, C], U32, name="xc_words", align_bytes=64)
+        xc_scales = keep.tile([P, C], U8, name="xc_scales", align_bytes=64)
+        nc.vector.tensor_copy(xq_scales[:], scales[:].indirect(offs_sb[:]))
+        nc.vector.tensor_copy(xc_scales[:], scales[:].indirect(cand_sb[:]))
+
+        w_bf = keep.tile([P, PACK, P, PACK], BF16, name="w_bf", align_bytes=64)
+        w_src = w_raw[:].rearrange("p j (m t) -> p m t j", t=PACK)
+        w_dst = w_bf[:].rearrange("p t m j -> p m t j")
+        nc.vector.tensor_copy(w_dst[:, :M_SPLIT], w_src[:, :M_SPLIT])
+        nc.scalar.copy(w_dst[:, M_SPLIT:], w_src[:, M_SPLIT:])
+        w_codes = keep.tile([P, H], U32, name="w_codes", align_bytes=64)
+        w_scales = keep.tile([P, H], U8, name="w_scales", align_bytes=64)
+        for u in range(2):
+            cols = slice(2 * P * u, 2 * P * (u + 1))
+            nc.vector.quantize_mx(
+                out=w_codes[:, cols].bitcast(FP8X4),
+                scales=w_scales[:, cols],
+                in_=w_bf[:, 2 * u : 2 * u + 2].rearrange("p t m j -> p (t m j)"),
+            )
+
+        nc.vector.tensor_copy(xq_words[:], words[:].indirect(offs_sb[:]))
+        y_rows = [keep.tile([P, S], F32, name=f"y_rows{t}") for t in range(PACK)]
+        y_psum = [psum.tile([P, S], F32, name=f"y_psum{t}") for t in range(PACK)]
+        for t in range(PACK):
+            cols = slice(P * t, P * (t + 1))
+            nc.tensor.matmul_mx(
+                out=y_psum[t][:],
+                lhsT=w_codes[:, cols].bitcast(FP8X4),
+                lhsT_scale=w_scales[:, cols],
+                rhs=xq_words[:].bitcast(FP8X4),
+                rhs_scale=xq_scales[:],
+                start=True,
+                stop=True,
+            )
+        half_c = C // 2
+        nc.vector.tensor_copy(xc_words[:, :half_c], words[:].indirect(cand_sb[:, : half_c // LANES]))
+        nc.scalar.copy(y_rows[0][:], y_psum[0][:])
+        for t in range(1, PACK):
+            nc.vector.tensor_copy(y_rows[t][:], y_psum[t][:])
+
+        z_codes = keep.tile([P, S], U32, name="z_codes", align_bytes=64)
+        z_scales = keep.tile([P, S], U8, name="z_scales", align_bytes=64)
+        s_psum = [psum.tile([P, S], F32, name=f"s_psum{c}") for c in range(C // P)]
+
+        def scores(c, cols):
+            rows = slice(P * c, P * (c + 1))
+            nc.tensor.matmul_mx(
+                out=s_psum[c][:, cols],
+                lhsT=xc_words[:, rows].bitcast(FP8X4),
+                lhsT_scale=xc_scales[:, rows],
+                rhs=z_codes[:, cols].bitcast(FP8X4),
+                rhs_scale=z_scales[:, cols],
+                start=True,
+                stop=True,
+            )
+
+        for h in range(2):
+            cols = slice(HALF * h, HALF * (h + 1))
+            entries = slice(HALF * h // LANES, HALF * (h + 1) // LANES)
+            z_bf = keep.tile([P, HALF, PACK], BF16, name=f"z_bf{h}", align_bytes=64)
+            for t in range(PACK):
+                y_n1 = ring.tile([P, HALF], F32, name="y_n1")
+                y_n2 = ring.tile([P, HALF], F32, name="y_n2")
+                nc.scalar.activation(y_n1[:], y_rows[t][:].indirect(n1_sb[:, entries]), COPY)
+                nc.scalar.activation(y_n2[:], y_rows[t][:].indirect(n2_sb[:, entries]), COPY)
+                least = ring.tile([P, HALF], F32, name="least")
+                diff = ring.tile([P, HALF], F32, name="diff")
+                nc.vector.tensor_tensor(least[:], y_n1[:], y_n2[:], ALU.min)
+                nc.vector.tensor_tensor(diff[:], y_rows[t][:, cols], least[:], ALU.subtract)
+                nc.vector.tensor_scalar(z_bf[:, :, t], diff[:], gain[:, t : t + 1], None, ALU.mult)
+            nc.vector.quantize_mx(
+                out=z_codes[:, cols].bitcast(FP8X4),
+                scales=z_scales[:, cols],
+                in_=z_bf[:].rearrange("p s t -> p (s t)"),
+            )
+            if h == 0:
+                nc.vector.tensor_copy(xc_words[:, half_c:], words[:].indirect(cand_sb[:, half_c // LANES :]))
+                for c in range(C // P):
+                    scores(c, cols)
+
+        first, second = slice(0, HALF), slice(HALF, S)
+        for c in range(C // P):
+            nc.scalar.activation(s_rows[c][:, first], s_psum[c][:, first], COPY, scale=0.0625)
+        for c in range(C // P):
+            scores(c, second)
+        nc.scalar.activation(s_rows[0][:, second], s_psum[0][:, second], COPY, scale=0.0625)
+        for c in range(1, C // P):
+            nc.vector.tensor_scalar(s_rows[c][:, second], s_psum[c][:, second], 0.0625, None, ALU.mult)
+
+        for c in range(C // P):
+            result = keep.tile([P, S], F32, name=f"result{c}")
+            last = c == C // P - 1
+            bounds = [0, 512, 768, 1024] if last else [0, 512, 1024]
+            for lo, hi in zip(bounds[:-1], bounds[1:]):
+                n = hi - lo
+                groups = n // MEMBERS
+                members = ring.tile([P, n], F32, name="members")
+                nc.scalar.activation(members[:], s_rows[c][:].indirect(n3_sb[:, lo // LANES : hi // LANES]), COPY)
+                pairs = members[:].rearrange("p (j u v) -> p j u v", u=2, v=2)
+                upper = ring.tile([P, groups, 2], F32, name="upper")
+                lower = ring.tile([P, groups, 2], F32, name="lower")
+                largest = ring.tile([P, groups], F32, name="largest")
+                smallest = ring.tile([P, groups], F32, name="smallest")
+                nc.vector.tensor_tensor(upper[:], pairs[:, :, 0, :], pairs[:, :, 1, :], ALU.max)
+                nc.vector.tensor_tensor(lower[:], pairs[:, :, 0, :], pairs[:, :, 1, :], ALU.min)
+                nc.vector.tensor_tensor(largest[:], upper[:, :, 0], upper[:, :, 1], ALU.max)
+                nc.vector.tensor_tensor(smallest[:], lower[:, :, 0], lower[:, :, 1], ALU.min)
+                cols = slice(lo // MEMBERS, hi // MEMBERS)
+                nc.vector.scalar_tensor_tensor(result[:, cols], smallest[:], -0.5, largest[:], ALU.mult, ALU.add)
+                if last:
+                    nc.sync.dma_start(out[P * c : P * (c + 1), cols], result[:, cols])
+            if not last:
+                nc.sync.dma_start(out[P * c : P * (c + 1), :], result[:])

@@ -37,51 +37,58 @@ def tile_picked_candundergspan_none_p_kernel(tc, x_words, x_scales, w1, gs, offs
         n2_sb = keep.tile([P, S // LANES], U16, name="n2_sb")
         n3_sb = keep.tile([P, W // LANES], U16, name="n3_sb")
         w_raw = keep.tile([P, PACK, H], F32, name="w_raw")
-        words = keep.tile([P, T], U32, name="words", align_bytes=64)
-        scales = keep.tile([P, T], U8, name="scales", align_bytes=64)
+        scales = keep.tile([P, T], U8, name="scales", tag="plane", align_bytes=64)
         gain = keep.tile([P, PACK], F32, name="gain")
 
         nc.vector.memset(scales[:].bitcast(I32), 0)
         nc.sync.dma_start(offs_sb[:], offs)
         nc.sync.dma_start(cand_sb[:], cand)
-        nc.sync.dma_start(w_raw[:], w1.rearrange("(p j) c -> p j c", j=PACK))
-        nc.sync.dma_start(words[:].bitcast(I32), x_words[0].rearrange("p n r -> p (n r)").bitcast(I32))
-        for q in range(4):
-            nc.scalar.dma_start(scales[32 * q : 32 * q + 4, :].bitcast(I32), x_scales[0][4 * q : 4 * q + 4, :].bitcast(I32))
         nc.sync.dma_start(n1_sb[:], n1)
+        nc.sync.dma_start(w_raw[:], w1.rearrange("(p j) c -> p j c", j=PACK))
         nc.sync.dma_start(n2_sb[:], n2)
-        nc.sync.dma_start(gain[:], gs.rearrange("(p t) o -> p (t o)", t=PACK))
         nc.sync.dma_start(n3_sb[:], n3)
+        nc.gpsimd.dma_start(gain[:], gs.rearrange("(p t) o -> p (t o)", t=PACK))
+        for q in range(4):
+            nc.sync.dma_start(scales[32 * q : 32 * q + 4, :].bitcast(I32), x_scales[0][4 * q : 4 * q + 4, :].bitcast(I32))
 
+        zeros = keep.tile([P, S_WINDOW - S], F32, name="zeros", tag="table", align_bytes=64)
+        nc.vector.memset(zeros[:], 0.0)
         s_rows = [keep.tile([P, S_WINDOW], F32, name=f"s_rows{c}") for c in range(C // P)]
         for c in range(C // P):
-            nc.gpsimd.memset(s_rows[c][:, S:], 0.0)
+            nc.vector.tensor_copy(s_rows[c][:, S:], zeros[:])
+        y_rows = [keep.tile([P, 2 * S if t < 2 else S], F32, name=f"y_rows{t}") for t in range(PACK)]
+        for t in range(2):
+            nc.vector.tensor_copy(y_rows[t][:, S:], zeros[:, :S])
+        words = keep.tile([P, T], U32, name="words", tag="table", align_bytes=64)
+        nc.sync.dma_start(words[:].bitcast(I32), x_words[0].rearrange("p n r -> p (n r)").bitcast(I32))
 
-        xq_words = keep.tile([P, S], U32, name="xq_words", align_bytes=64)
         xq_scales = keep.tile([P, S], U8, name="xq_scales", align_bytes=64)
-        xc_words = keep.tile([P, C], U32, name="xc_words", align_bytes=64)
-        xc_scales = keep.tile([P, C], U8, name="xc_scales", align_bytes=64)
-        nc.vector.tensor_copy(xq_scales[:], scales[:].indirect(offs_sb[:]))
-        nc.vector.tensor_copy(xc_scales[:], scales[:].indirect(cand_sb[:]))
+        scales_again = keep.tile([P, T], U8, name="scales_again", align_bytes=64)
 
-        w_bf = keep.tile([P, PACK, P, PACK], BF16, name="w_bf", align_bytes=64)
-        w_src = w_raw[:].rearrange("p j (m t) -> p m t j", t=PACK)
-        w_dst = w_bf[:].rearrange("p t m j -> p m t j")
-        nc.vector.tensor_copy(w_dst[:, :M_SPLIT], w_src[:, :M_SPLIT])
-        nc.scalar.copy(w_dst[:, M_SPLIT:], w_src[:, M_SPLIT:])
-        w_codes = keep.tile([P, H], U32, name="w_codes", align_bytes=64)
-        w_scales = keep.tile([P, H], U8, name="w_scales", align_bytes=64)
-        for u in range(2):
+        w_bf = [keep.tile([P, 2, P, PACK], BF16, name=f"w_bf{u}", tag=f"stage{u}", align_bytes=64) for u in range(2)]
+        w_src = w_raw[:].rearrange("p j (m u i) -> p u m j i", u=2, i=2)
+        w_dst = [w_bf[u][:].rearrange("p i m j -> p m j i") for u in range(2)]
+        nc.scalar.copy(w_dst[0], w_src[:, 0])
+        nc.vector.tensor_copy(w_dst[1][:, :M_SPLIT], w_src[:, 1, :M_SPLIT])
+        nc.scalar.copy(w_dst[1][:, M_SPLIT:], w_src[:, 1, M_SPLIT:])
+        nc.vector.tensor_copy(xq_scales[:], scales[:].indirect(offs_sb[:]))
+        nc.vector.tensor_copy(scales_again[:].bitcast(I32), scales[:].bitcast(I32))
+        w_codes = keep.tile([P, H], U32, name="w_codes", tag="codes", align_bytes=64)
+        w_scales = keep.tile([P, H], U8, name="w_scales", tag="plane", align_bytes=64)
+
+        def quantize_w(u):
             cols = slice(2 * P * u, 2 * P * (u + 1))
             nc.vector.quantize_mx(
                 out=w_codes[:, cols].bitcast(FP8X4),
                 scales=w_scales[:, cols],
-                in_=w_bf[:, 2 * u : 2 * u + 2].rearrange("p t m j -> p (t m j)"),
+                in_=w_bf[u][:].rearrange("p i m j -> p (i m j)"),
             )
 
+        quantize_w(0)
+        xq_words = keep.tile([P, S], U32, name="xq_words", tag="stage0", align_bytes=64)
         nc.vector.tensor_copy(xq_words[:], words[:].indirect(offs_sb[:]))
-        y_rows = [keep.tile([P, S], F32, name=f"y_rows{t}") for t in range(PACK)]
-        y_psum = [psum.tile([P, S], F32, name=f"y_psum{t}") for t in range(PACK)]
+        quantize_w(1)
+        y_psum = [psum.tile([P, S], F32, name=f"y_psum{t}", tag=f"bank{t}") for t in range(PACK)]
         for t in range(PACK):
             cols = slice(P * t, P * (t + 1))
             nc.tensor.matmul_mx(
@@ -94,81 +101,131 @@ def tile_picked_candundergspan_none_p_kernel(tc, x_words, x_scales, w1, gs, offs
                 stop=True,
             )
         half_c = C // 2
-        nc.vector.tensor_copy(xc_words[:, :half_c], words[:].indirect(cand_sb[:, : half_c // LANES]))
-        nc.scalar.copy(y_rows[0][:], y_psum[0][:])
+        nc.scalar.copy(y_rows[0][:, :S], y_psum[0][:])
         for t in range(1, PACK):
-            nc.vector.tensor_copy(y_rows[t][:], y_psum[t][:])
+            nc.vector.tensor_copy(y_rows[t][:, :S], y_psum[t][:])
+        xc_scales = keep.tile([P, C], U8, name="xc_scales", tag="plane", align_bytes=64)
+        nc.vector.tensor_copy(xc_scales[:], scales_again[:].indirect(cand_sb[:]))
+        xc_words = [
+            keep.tile([P, half_c], U32, name="xc_words0", tag="stage1", align_bytes=64),
+            keep.tile([P, half_c], U32, name="xc_words1", tag="codes", align_bytes=64),
+        ]
+        nc.vector.tensor_copy(xc_words[0][:], words[:].indirect(cand_sb[:, : half_c // LANES]))
+        nc.vector.tensor_copy(xc_words[1][:], words[:].indirect(cand_sb[:, half_c // LANES :]))
 
         z_codes = keep.tile([P, S], U32, name="z_codes", align_bytes=64)
         z_scales = keep.tile([P, S], U8, name="z_scales", align_bytes=64)
-        s_psum = [psum.tile([P, S], F32, name=f"s_psum{c}") for c in range(C // P)]
+        y_n1 = keep.tile([P, PACK, S], F32, name="y_n1")
+        y_n2 = keep.tile([P, PACK, S], F32, name="y_n2")
+        least = keep.tile([P, PACK, S], F32, name="least")
+        quarter = HALF // 2
+        pieces = [(0, HALF), (HALF, HALF + quarter), (HALF + quarter, S)]
+        diff = {lo: keep.tile([P, PACK, hi - lo], F32, name=f"diff{lo}") for lo, hi in pieces}
+        z_bf = {lo: keep.tile([P, hi - lo, PACK], BF16, name=f"z_bf{lo}", align_bytes=64) for lo, hi in pieces}
 
-        def scores(c, cols):
+        def fetch(t, lo, hi):
+            entries = slice(lo // LANES, hi // LANES)
+            nc.scalar.activation(y_n1[:, t, lo:hi], y_rows[t][:].indirect(n1_sb[:, entries]), COPY)
+            nc.scalar.activation(y_n2[:, t, lo:hi], y_rows[t][:].indirect(n2_sb[:, entries]), COPY)
+
+        def differ(t, lo, hi):
+            nc.vector.tensor_tensor(least[:, t, lo:hi], y_n1[:, t, lo:hi], y_n2[:, t, lo:hi], ALU.min)
+            for u, v in [(u, v) for u, v in pieces if lo <= u < hi]:
+                nc.vector.tensor_tensor(diff[u][:, t, :], y_rows[t][:, u:v], least[:, t, u:v], ALU.subtract)
+
+        def quantize_z(lo, hi):
+            n = hi - lo
+            nc.vector.tensor_tensor(
+                z_bf[lo][:].rearrange("p (s i) t -> p s t i", i=2),
+                diff[lo][:].rearrange("p t (s i) -> p s t i", i=2),
+                gain[:].unsqueeze(1).unsqueeze(3).to_broadcast([P, n // 2, PACK, 2]),
+                ALU.mult,
+            )
+            nc.vector.quantize_mx(
+                out=z_codes[:, lo:hi].bitcast(FP8X4),
+                scales=z_scales[:, lo:hi],
+                in_=z_bf[lo][:].rearrange("p s t -> p (s t)"),
+            )
+
+        def scores(c, lo, hi, acc):
             rows = slice(P * c, P * (c + 1))
             nc.tensor.matmul_mx(
-                out=s_psum[c][:, cols],
-                lhsT=xc_words[:, rows].bitcast(FP8X4),
+                out=acc,
+                lhsT=xc_words[c // 2][:, P * (c % 2) : P * (c % 2 + 1)].bitcast(FP8X4),
                 lhsT_scale=xc_scales[:, rows],
-                rhs=z_codes[:, cols].bitcast(FP8X4),
-                rhs_scale=z_scales[:, cols],
+                rhs=z_codes[:, lo:hi].bitcast(FP8X4),
+                rhs_scale=z_scales[:, lo:hi],
                 start=True,
                 stop=True,
             )
 
-        for h in range(2):
-            cols = slice(HALF * h, HALF * (h + 1))
-            entries = slice(HALF * h // LANES, HALF * (h + 1) // LANES)
-            z_bf = keep.tile([P, HALF, PACK], BF16, name=f"z_bf{h}", align_bytes=64)
-            for t in range(PACK):
-                y_n1 = ring.tile([P, HALF], F32, name="y_n1")
-                y_n2 = ring.tile([P, HALF], F32, name="y_n2")
-                nc.scalar.activation(y_n1[:], y_rows[t][:].indirect(n1_sb[:, entries]), COPY)
-                nc.scalar.activation(y_n2[:], y_rows[t][:].indirect(n2_sb[:, entries]), COPY)
-                least = ring.tile([P, HALF], F32, name="least")
-                diff = ring.tile([P, HALF], F32, name="diff")
-                nc.vector.tensor_tensor(least[:], y_n1[:], y_n2[:], ALU.min)
-                nc.vector.tensor_tensor(diff[:], y_rows[t][:, cols], least[:], ALU.subtract)
-                nc.vector.tensor_scalar(z_bf[:, :, t], diff[:], gain[:, t : t + 1], None, ALU.mult)
-            nc.vector.quantize_mx(
-                out=z_codes[:, cols].bitcast(FP8X4),
-                scales=z_scales[:, cols],
-                in_=z_bf[:].rearrange("p s t -> p (s t)"),
-            )
-            if h == 0:
-                nc.vector.tensor_copy(xc_words[:, half_c:], words[:].indirect(cand_sb[:, half_c // LANES :]))
-                for c in range(C // P):
-                    scores(c, cols)
+        steps = [(0, 0, S), (1, 0, S), (2, 0, HALF), (3, 0, HALF), (2, HALF, S), (3, *pieces[1]), (3, *pieces[2])]
+        for step in steps:
+            fetch(*step)
+        for t, lo, hi in steps:
+            differ(t, lo, hi)
+            if t == PACK - 1:
+                quantize_z(lo, hi)
 
-        first, second = slice(0, HALF), slice(HALF, S)
+        s_first = [psum.tile([P, HALF], F32, name=f"s_first{c}") for c in range(C // P)]
         for c in range(C // P):
-            nc.scalar.activation(s_rows[c][:, first], s_psum[c][:, first], COPY, scale=0.0625)
+            scores(c, 0, HALF, s_first[c][:])
+        s_third = psum.tile([P, quarter], F32, name="s_third", tag="bank0")
+        s_fourth = psum.tile([P, quarter], F32, name="s_fourth", tag="bank1")
+        s_second1 = psum.tile([P, HALF], F32, name="s_second1", tag="bank2")
+        s_second23 = psum.tile([P, 2, HALF], F32, name="s_second23", tag="bank3")
+        scores(0, HALF, HALF + quarter, s_third[:])
+        scores(0, HALF + quarter, S, s_fourth[:])
+        scores(1, HALF, S, s_second1[:])
+        scores(2, HALF, S, s_second23[:, 0, :])
+        scores(3, HALF, S, s_second23[:, 1, :])
         for c in range(C // P):
-            scores(c, second)
-        nc.scalar.activation(s_rows[0][:, second], s_psum[0][:, second], COPY, scale=0.0625)
-        for c in range(1, C // P):
-            nc.vector.tensor_scalar(s_rows[c][:, second], s_psum[c][:, second], 0.0625, None, ALU.mult)
+            nc.scalar.activation(s_rows[c][:, :HALF], s_first[c][:], COPY, scale=0.0625)
+        nc.scalar.activation(s_rows[0][:, HALF : HALF + quarter], s_third[:], COPY, scale=0.0625)
+        nc.scalar.activation(s_rows[0][:, HALF + quarter : S], s_fourth[:], COPY, scale=0.0625)
+        nc.vector.tensor_scalar(s_rows[1][:, HALF:S], s_second1[:], 0.0625, None, ALU.mult)
+        for c in (2, 3):
+            nc.vector.tensor_scalar(s_rows[c][:, HALF:S], s_second23[:, c - 2, :], 0.0625, None, ALU.mult)
 
+        def finish(c, cols, largest, smallest, result):
+            nc.vector.scalar_tensor_tensor(result[:, cols], smallest[:], -0.5, largest[:], ALU.mult, ALU.add)
+            nc.sync.dma_start(out[P * c : P * (c + 1), cols], result[:, cols])
+
+        pending = None
         for c in range(C // P):
             result = keep.tile([P, S], F32, name=f"result{c}")
             last = c == C // P - 1
-            bounds = [0, 512, 768, 1024] if last else [0, 512, 1024]
-            for lo, hi in zip(bounds[:-1], bounds[1:]):
-                n = hi - lo
-                groups = n // MEMBERS
-                members = ring.tile([P, n], F32, name="members")
-                nc.scalar.activation(members[:], s_rows[c][:].indirect(n3_sb[:, lo // LANES : hi // LANES]), COPY)
-                pairs = members[:].rearrange("p (j u v) -> p j u v", u=2, v=2)
-                upper = ring.tile([P, groups, 2], F32, name="upper")
-                lower = ring.tile([P, groups, 2], F32, name="lower")
+            if last:
+                stretches = [[0, 512], [512, 768], [768, 896], [896, 1024]]
+            else:
+                stretches = [[0, 256, 512, 1024]] if c == 0 else [[0, 512, 1024]]
+            for bounds in stretches:
+                base, groups = bounds[0], (bounds[-1] - bounds[0]) // MEMBERS
                 largest = ring.tile([P, groups], F32, name="largest")
                 smallest = ring.tile([P, groups], F32, name="smallest")
-                nc.vector.tensor_tensor(upper[:], pairs[:, :, 0, :], pairs[:, :, 1, :], ALU.max)
-                nc.vector.tensor_tensor(lower[:], pairs[:, :, 0, :], pairs[:, :, 1, :], ALU.min)
-                nc.vector.tensor_tensor(largest[:], upper[:, :, 0], upper[:, :, 1], ALU.max)
-                nc.vector.tensor_tensor(smallest[:], lower[:, :, 0], lower[:, :, 1], ALU.min)
-                cols = slice(lo // MEMBERS, hi // MEMBERS)
-                nc.vector.scalar_tensor_tensor(result[:, cols], smallest[:], -0.5, largest[:], ALU.mult, ALU.add)
-                if last:
-                    nc.sync.dma_start(out[P * c : P * (c + 1), cols], result[:, cols])
-            if not last:
-                nc.sync.dma_start(out[P * c : P * (c + 1), :], result[:])
+                by_reduce = groups == 32
+                if not by_reduce:
+                    upper = ring.tile([P, groups, 2], F32, name="upper")
+                    lower = ring.tile([P, groups, 2], F32, name="lower")
+                for lo, hi in zip(bounds[:-1], bounds[1:]):
+                    members = ring.tile([P, hi - lo], F32, name="members")
+                    nc.scalar.activation(members[:], s_rows[c][:].indirect(n3_sb[:, lo // LANES : hi // LANES]), COPY)
+                    if by_reduce:
+                        quads = members[:].rearrange("p (j u) -> p j u", u=MEMBERS)
+                        nc.vector.tensor_reduce(largest[:], quads, mybir.AxisListType.X, ALU.max)
+                    else:
+                        pairs = members[:].rearrange("p (j u v) -> p j u v", u=2, v=2)
+                        js = slice((lo - base) // MEMBERS, (hi - base) // MEMBERS)
+                        nc.vector.tensor_tensor(upper[:, js, :], pairs[:, :, 0, :], pairs[:, :, 1, :], ALU.max)
+                    if pending is not None:
+                        finish(*pending)
+                        pending = None
+                    if by_reduce:
+                        nc.vector.tensor_reduce(smallest[:], quads, mybir.AxisListType.X, ALU.min)
+                    else:
+                        nc.vector.tensor_tensor(lower[:, js, :], pairs[:, :, 0, :], pairs[:, :, 1, :], ALU.min)
+                if not by_reduce:
+                    nc.vector.tensor_tensor(largest[:], upper[:, :, 0], upper[:, :, 1], ALU.max)
+                    nc.vector.tensor_tensor(smallest[:], lower[:, :, 0], lower[:, :, 1], ALU.min)
+                pending = (c, slice(base // MEMBERS, base // MEMBERS + groups), largest, smallest, result)
+        finish(*pending)

@@ -36,9 +36,8 @@ def tile_picked_candundergspan_none_p_kernel(tc, x_words, x_scales, w1, gs, offs
         n1_sb = keep.tile([P, S // LANES], U16, name="n1_sb")
         n2_sb = keep.tile([P, S // LANES], U16, name="n2_sb")
         n3_sb = keep.tile([P, W // LANES], U16, name="n3_sb")
-        w_raw = keep.tile([P, PACK, H], F32, name="w_raw")
+        w_raw = keep.tile([P, PACK, H], F32, name="w_raw", tag="raw")
         scales = keep.tile([P, T], U8, name="scales", tag="plane", align_bytes=64)
-        gain = keep.tile([P, PACK], F32, name="gain")
 
         nc.vector.memset(scales[:].bitcast(I32), 0)
         nc.sync.dma_start(offs_sb[:], offs)
@@ -47,7 +46,6 @@ def tile_picked_candundergspan_none_p_kernel(tc, x_words, x_scales, w1, gs, offs
         nc.sync.dma_start(w_raw[:], w1.rearrange("(p j) c -> p j c", j=PACK))
         nc.sync.dma_start(n2_sb[:], n2)
         nc.sync.dma_start(n3_sb[:], n3)
-        nc.gpsimd.dma_start(gain[:], gs.rearrange("(p t) o -> p (t o)", t=PACK))
         for q in range(4):
             nc.sync.dma_start(scales[32 * q : 32 * q + 4, :].bitcast(I32), x_scales[0][4 * q : 4 * q + 4, :].bitcast(I32))
 
@@ -71,6 +69,8 @@ def tile_picked_candundergspan_none_p_kernel(tc, x_words, x_scales, w1, gs, offs
         nc.scalar.copy(w_dst[0], w_src[:, 0])
         nc.vector.tensor_copy(w_dst[1][:, :M_SPLIT], w_src[:, 1, :M_SPLIT])
         nc.scalar.copy(w_dst[1][:, M_SPLIT:], w_src[:, 1, M_SPLIT:])
+        gain = keep.tile([P, PACK], F32, name="gain", tag="raw")
+        nc.sync.dma_start(gain[:], gs.rearrange("(p t) o -> p (t o)", t=PACK))
         nc.vector.tensor_copy(xq_scales[:], scales[:].indirect(offs_sb[:]))
         nc.vector.tensor_copy(scales_again[:].bitcast(I32), scales[:].bitcast(I32))
         w_codes = keep.tile([P, H], U32, name="w_codes", tag="codes", align_bytes=64)
@@ -88,63 +88,81 @@ def tile_picked_candundergspan_none_p_kernel(tc, x_words, x_scales, w1, gs, offs
         xq_words = keep.tile([P, S], U32, name="xq_words", tag="stage0", align_bytes=64)
         nc.vector.tensor_copy(xq_words[:], words[:].indirect(offs_sb[:]))
         quantize_w(1)
-        y_psum = [psum.tile([P, S], F32, name=f"y_psum{t}", tag=f"bank{t}") for t in range(PACK)]
-        for t in range(PACK):
+
+        def project(t, lo, hi, acc):
             cols = slice(P * t, P * (t + 1))
             nc.tensor.matmul_mx(
-                out=y_psum[t][:],
+                out=acc,
                 lhsT=w_codes[:, cols].bitcast(FP8X4),
                 lhsT_scale=w_scales[:, cols],
-                rhs=xq_words[:].bitcast(FP8X4),
-                rhs_scale=xq_scales[:],
+                rhs=xq_words[:, lo:hi].bitcast(FP8X4),
+                rhs_scale=xq_scales[:, lo:hi],
                 start=True,
                 stop=True,
             )
-        half_c = C // 2
-        nc.scalar.copy(y_rows[0][:, :S], y_psum[0][:])
+
+        for h in range(2):
+            y_half = psum.tile([P, HALF], F32, name=f"y_half{h}")
+            project(0, HALF * h, HALF * (h + 1), y_half[:])
+            nc.scalar.copy(y_rows[0][:, HALF * h : HALF * (h + 1)], y_half[:])
         for t in range(1, PACK):
-            nc.vector.tensor_copy(y_rows[t][:, :S], y_psum[t][:])
+            y_psum = psum.tile([P, S], F32, name=f"y_psum{t}", tag=f"bank{t}")
+            project(t, 0, S, y_psum[:])
+            nc.vector.tensor_copy(y_rows[t][:, :S], y_psum[:])
+        half_c = C // 2
         xc_scales = keep.tile([P, C], U8, name="xc_scales", tag="plane", align_bytes=64)
         nc.vector.tensor_copy(xc_scales[:], scales_again[:].indirect(cand_sb[:]))
         xc_words = [
             keep.tile([P, half_c], U32, name="xc_words0", tag="stage1", align_bytes=64),
-            keep.tile([P, half_c], U32, name="xc_words1", tag="codes", align_bytes=64),
         ]
         nc.vector.tensor_copy(xc_words[0][:], words[:].indirect(cand_sb[:, : half_c // LANES]))
-        nc.vector.tensor_copy(xc_words[1][:], words[:].indirect(cand_sb[:, half_c // LANES :]))
 
         z_codes = keep.tile([P, S], U32, name="z_codes", align_bytes=64)
         z_scales = keep.tile([P, S], U8, name="z_scales", align_bytes=64)
         y_n1 = keep.tile([P, PACK, S], F32, name="y_n1")
         y_n2 = keep.tile([P, PACK, S], F32, name="y_n2")
-        least = keep.tile([P, PACK, S], F32, name="least")
-        quarter = HALF // 2
-        pieces = [(0, HALF), (HALF, HALF + quarter), (HALF + quarter, S)]
-        diff = {lo: keep.tile([P, PACK, hi - lo], F32, name=f"diff{lo}") for lo, hi in pieces}
-        z_bf = {lo: keep.tile([P, hi - lo, PACK], BF16, name=f"z_bf{lo}", align_bytes=64) for lo, hi in pieces}
+        least = keep.tile([P, PACK - 1, S], F32, name="least")
+        diff = keep.tile([P, 2, PACK - 1, HALF], F32, name="diff")
+        z_bf = [keep.tile([P, HALF, PACK], BF16, name=f"z_bf{h}", tag=f"z_stage{h}", align_bytes=64) for h in range(2)]
+        first, second, every = slice(0, HALF), slice(HALF, S), slice(0, S)
 
-        def fetch(t, lo, hi):
-            entries = slice(lo // LANES, hi // LANES)
-            nc.scalar.activation(y_n1[:, t, lo:hi], y_rows[t][:].indirect(n1_sb[:, entries]), COPY)
-            nc.scalar.activation(y_n2[:, t, lo:hi], y_rows[t][:].indirect(n2_sb[:, entries]), COPY)
+        def fetch(t, cols):
+            entries = slice(cols.start // LANES, cols.stop // LANES)
+            nc.scalar.activation(y_n1[:, t, cols], y_rows[t][:].indirect(n1_sb[:, entries]), COPY)
+            nc.scalar.activation(y_n2[:, t, cols], y_rows[t][:].indirect(n2_sb[:, entries]), COPY)
 
-        def differ(t, lo, hi):
-            nc.vector.tensor_tensor(least[:, t, lo:hi], y_n1[:, t, lo:hi], y_n2[:, t, lo:hi], ALU.min)
-            for u, v in [(u, v) for u, v in pieces if lo <= u < hi]:
-                nc.vector.tensor_tensor(diff[u][:, t, :], y_rows[t][:, u:v], least[:, t, u:v], ALU.subtract)
+        def smaller(t, cols, into):
+            nc.vector.tensor_tensor(into, y_n1[:, t, cols], y_n2[:, t, cols], ALU.min)
 
-        def quantize_z(lo, hi):
-            n = hi - lo
+        def differ(t, cols):
+            h = cols.start // HALF
+            into = diff[:, :, t, :] if cols is every else diff[:, h, t, :]
+            rows = y_rows[t][:, cols]
+            smallest = least[:, t, cols]
+            if cols is every:
+                rows = rows.rearrange("p (h s) -> p h s", h=2)
+                smallest = smallest.rearrange("p (h s) -> p h s", h=2)
+            nc.vector.tensor_tensor(into, rows, smallest, ALU.subtract)
+
+        def last_plane(h, smallest):
+            nc.vector.scalar_tensor_tensor(
+                z_bf[h][:, :, 3], smallest, minus_gain[:], weighted[:, HALF * h : HALF * (h + 1)], ALU.mult, ALU.add
+            )
+
+        def weigh(h, planes):
             nc.vector.tensor_tensor(
-                z_bf[lo][:].rearrange("p (s i) t -> p s t i", i=2),
-                diff[lo][:].rearrange("p t (s i) -> p s t i", i=2),
-                gain[:].unsqueeze(1).unsqueeze(3).to_broadcast([P, n // 2, PACK, 2]),
+                z_bf[h][:, :, :planes].rearrange("p (s i) t -> p s t i", i=2),
+                diff[:, h].rearrange("p t (s i) -> p s t i", i=2),
+                gain[:, :planes].unsqueeze(1).unsqueeze(3).to_broadcast([P, HALF // 2, planes, 2]),
                 ALU.mult,
             )
+
+        def quantize_z(h):
+            cols = slice(HALF * h, HALF * (h + 1))
             nc.vector.quantize_mx(
-                out=z_codes[:, lo:hi].bitcast(FP8X4),
-                scales=z_scales[:, lo:hi],
-                in_=z_bf[lo][:].rearrange("p s t -> p (s t)"),
+                out=z_codes[:, cols].bitcast(FP8X4),
+                scales=z_scales[:, cols],
+                in_=z_bf[h][:].rearrange("p s t -> p (s t)"),
             )
 
         def scores(c, lo, hi, acc):
@@ -159,33 +177,39 @@ def tile_picked_candundergspan_none_p_kernel(tc, x_words, x_scales, w1, gs, offs
                 stop=True,
             )
 
-        steps = [(0, 0, S), (1, 0, S), (2, 0, HALF), (3, 0, HALF), (2, HALF, S), (3, *pieces[1]), (3, *pieces[2])]
-        for step in steps:
-            fetch(*step)
-        for t, lo, hi in steps:
-            differ(t, lo, hi)
-            if t == PACK - 1:
-                quantize_z(lo, hi)
+        for t, cols in [(0, every), (1, every), (2, first), (2, second), (3, first), (3, second)]:
+            fetch(t, cols)
 
-        s_first = [psum.tile([P, HALF], F32, name=f"s_first{c}") for c in range(C // P)]
-        for c in range(C // P):
-            scores(c, 0, HALF, s_first[c][:])
-        s_third = psum.tile([P, quarter], F32, name="s_third", tag="bank0")
-        s_fourth = psum.tile([P, quarter], F32, name="s_fourth", tag="bank1")
-        s_second1 = psum.tile([P, HALF], F32, name="s_second1", tag="bank2")
-        s_second23 = psum.tile([P, 2, HALF], F32, name="s_second23", tag="bank3")
-        scores(0, HALF, HALF + quarter, s_third[:])
-        scores(0, HALF + quarter, S, s_fourth[:])
-        scores(1, HALF, S, s_second1[:])
-        scores(2, HALF, S, s_second23[:, 0, :])
-        scores(3, HALF, S, s_second23[:, 1, :])
-        for c in range(C // P):
-            nc.scalar.activation(s_rows[c][:, :HALF], s_first[c][:], COPY, scale=0.0625)
-        nc.scalar.activation(s_rows[0][:, HALF : HALF + quarter], s_third[:], COPY, scale=0.0625)
-        nc.scalar.activation(s_rows[0][:, HALF + quarter : S], s_fourth[:], COPY, scale=0.0625)
-        nc.vector.tensor_scalar(s_rows[1][:, HALF:S], s_second1[:], 0.0625, None, ALU.mult)
-        for c in (2, 3):
-            nc.vector.tensor_scalar(s_rows[c][:, HALF:S], s_second23[:, c - 2, :], 0.0625, None, ALU.mult)
+        weighted = keep.tile([P, S], F32, name="weighted")
+        minus_gain = keep.tile([P, 1], F32, name="minus_gain")
+        nc.vector.tensor_scalar(minus_gain[:], gain[:, 3:4], -1.0, None, ALU.mult)
+        nc.vector.tensor_scalar(weighted[:], y_rows[3][:], gain[:, 3:4], None, ALU.mult)
+        for t in range(2):
+            smaller(t, every, least[:, t, :])
+            differ(t, every)
+        smaller(2, first, least[:, 2, first])
+        differ(2, first)
+        smaller(2, second, least[:, 2, second])
+        weigh(0, PACK - 1)
+        differ(2, second)
+        smaller(3, first, least[:, 2, second])
+        weigh(1, PACK - 1)
+        last_plane(0, least[:, 2, second])
+        smaller(3, second, diff[:, 1, 2, :])
+        quantize_z(0)
+        last_plane(1, diff[:, 1, 2, :])
+        quantize_z(1)
+        xc_words.append(keep.tile([P, half_c], U32, name="xc_words1", tag="z_stage1", align_bytes=64))
+        nc.vector.tensor_copy(xc_words[1][:], words[:].indirect(cand_sb[:, half_c // LANES :]))
+
+        s_halves = [psum.tile([P, HALF], F32, name=f"s_half{h}") for h in range(2)]
+        for h, cols in enumerate((first, second)):
+            scores(0, cols.start, cols.stop, s_halves[h][:])
+            nc.scalar.activation(s_rows[0][:, cols], s_halves[h][:], COPY, scale=0.0625)
+        for c in range(1, C // P):
+            s_psum = psum.tile([P, S], F32, name=f"s_psum{c}", tag=f"bank{c}")
+            scores(c, 0, S, s_psum[:])
+            nc.vector.tensor_scalar(s_rows[c][:, :S], s_psum[:], 0.0625, None, ALU.mult)
 
         def finish(c, cols, largest, smallest, result):
             nc.vector.scalar_tensor_tensor(result[:, cols], smallest[:], -0.5, largest[:], ALU.mult, ALU.add)
@@ -198,7 +222,7 @@ def tile_picked_candundergspan_none_p_kernel(tc, x_words, x_scales, w1, gs, offs
             if last:
                 stretches = [[0, 512], [512, 768], [768, 896], [896, 1024]]
             else:
-                stretches = [[0, 256, 512, 1024]] if c == 0 else [[0, 512, 1024]]
+                stretches = [[0, 512, 1024]]
             for bounds in stretches:
                 base, groups = bounds[0], (bounds[-1] - bounds[0]) // MEMBERS
                 largest = ring.tile([P, groups], F32, name="largest")

@@ -222,7 +222,7 @@ def tile_picked_candundergspan_none_p_kernel(tc, x_words, x_scales, w1, gs, offs
             if last:
                 stretches = [[0, 512], [512, 768], [768, 896], [896, 1024]]
             else:
-                stretches = [[0, 512, 1024]]
+                stretches = [[[0, 256, 512, 1024]], [[0, 512, 1024]], [[0, 512], [512, 1024]]][c]
             for bounds in stretches:
                 base, groups = bounds[0], (bounds[-1] - bounds[0]) // MEMBERS
                 largest = ring.tile([P, groups], F32, name="largest")

from contextlib import ExitStack

import concourse.mybir as mybir

K, T, S, H, C, W = 512, 2048, 256, 512, 512, 1024
FLOPS = 2 * K * H * S + 2 * K * C * S

F32 = mybir.dt.float32
BF16 = mybir.dt.bfloat16
I32 = mybir.dt.int32
U32 = mybir.dt.uint32
U16 = mybir.dt.uint16
U8 = mybir.dt.uint8
FP8X4 = mybir.dt.float8_e4m3fn_x4
ALU = mybir.AluOpType
COPY = mybir.ActivationFunctionType.Copy

P = 128
PACK = 4
LANES = 16
MEMBERS = 4
HALF = S // 2
S_WINDOW = 528
M_SPLIT = 64


def tile_picked_candundergspan_none_p_kernel(tc, x_words, x_scales, w1, gs, offs, n1, n2, cand, n3, out):
    nc = tc.nc
    with ExitStack() as ctx:
        keep = ctx.enter_context(tc.tile_pool(name="keep", bufs=1))
        ring = ctx.enter_context(tc.tile_pool(name="ring", bufs=3))
        psum = ctx.enter_context(tc.psum_pool(name="psum", bufs=1))

        offs_sb = keep.tile([P, S // LANES], U16, name="offs_sb")
        cand_sb = keep.tile([P, C // LANES], U16, name="cand_sb")
        n1_sb = keep.tile([P, S // LANES], U16, name="n1_sb")
        n2_sb = keep.tile([P, S // LANES], U16, name="n2_sb")
        n3_sb = keep.tile([P, W // LANES], U16, name="n3_sb")
        w_raw = keep.tile([P, PACK, H], F32, name="w_raw", tag="raw")
        scales = keep.tile([P, T], U8, name="scales", tag="plane", align_bytes=64)

        nc.vector.memset(scales[:].bitcast(I32), 0)
        nc.sync.dma_start(offs_sb[:], offs)
        nc.sync.dma_start(cand_sb[:], cand)
        nc.sync.dma_start(n1_sb[:], n1)
        nc.sync.dma_start(w_raw[:], w1.rearrange("(p j) c -> p j c", j=PACK))
        nc.sync.dma_start(n2_sb[:], n2)
        nc.sync.dma_start(n3_sb[:], n3)
        for q in range(4):
            nc.sync.dma_start(scales[32 * q : 32 * q + 4, :].bitcast(I32), x_scales[0][4 * q : 4 * q + 4, :].bitcast(I32))

        zeros = keep.tile([P, S_WINDOW - S], F32, name="zeros", tag="table", align_bytes=64)
        nc.vector.memset(zeros[:], 0.0)
        s_rows = [keep.tile([P, S_WINDOW], F32, name=f"s_rows{c}") for c in range(C // P)]
        for c in range(C // P):
            nc.vector.tensor_copy(s_rows[c][:, S:], zeros[:])
        y_rows = [keep.tile([P, 2 * S if t < 2 else S], F32, name=f"y_rows{t}") for t in range(PACK)]
        for t in range(2):
            nc.vector.tensor_copy(y_rows[t][:, S:], zeros[:, :S])
        words = keep.tile([P, T], U32, name="words", tag="table", align_bytes=64)
        nc.sync.dma_start(words[:].bitcast(I32), x_words[0].rearrange("p n r -> p (n r)").bitcast(I32))

        xq_scales = keep.tile([P, S], U8, name="xq_scales", align_bytes=64)
        scales_again = keep.tile([P, T], U8, name="scales_again", align_bytes=64)

        w_bf = [keep.tile([P, 2, P, PACK], BF16, name=f"w_bf{u}", tag=f"stage{u}", align_bytes=64) for u in range(2)]
        w_src = w_raw[:].rearrange("p j (m u i) -> p u m j i", u=2, i=2)
        w_dst = [w_bf[u][:].rearrange("p i m j -> p m j i") for u in range(2)]
        nc.scalar.copy(w_dst[0], w_src[:, 0])
        nc.vector.tensor_copy(w_dst[1][:, :M_SPLIT], w_src[:, 1, :M_SPLIT])
        nc.scalar.copy(w_dst[1][:, M_SPLIT:], w_src[:, 1, M_SPLIT:])
        gain = keep.tile([P, PACK], F32, name="gain", tag="raw")
        nc.sync.dma_start(gain[:], gs.rearrange("(p t) o -> p (t o)", t=PACK))
        nc.vector.tensor_copy(xq_scales[:], scales[:].indirect(offs_sb[:]))
        nc.vector.tensor_copy(scales_again[:].bitcast(I32), scales[:].bitcast(I32))
        w_codes = keep.tile([P, H], U32, name="w_codes", tag="codes", align_bytes=64)
        w_scales = keep.tile([P, H], U8, name="w_scales", tag="plane", align_bytes=64)

        def quantize_w(u):
            cols = slice(2 * P * u, 2 * P * (u + 1))
            nc.vector.quantize_mx(
                out=w_codes[:, cols].bitcast(FP8X4),
                scales=w_scales[:, cols],
                in_=w_bf[u][:].rearrange("p i m j -> p (i m j)"),
            )

        quantize_w(0)
        xq_words = keep.tile([P, S], U32, name="xq_words", tag="stage0", align_bytes=64)
        nc.vector.tensor_copy(xq_words[:], words[:].indirect(offs_sb[:]))
        quantize_w(1)

        def project(t, lo, hi, acc):
            cols = slice(P * t, P * (t + 1))
            nc.tensor.matmul_mx(
                out=acc,
                lhsT=w_codes[:, cols].bitcast(FP8X4),
                lhsT_scale=w_scales[:, cols],
                rhs=xq_words[:, lo:hi].bitcast(FP8X4),
                rhs_scale=xq_scales[:, lo:hi],
                start=True,
                stop=True,
            )

        for h in range(2):
            y_half = psum.tile([P, HALF], F32, name=f"y_half{h}")
            project(0, HALF * h, HALF * (h + 1), y_half[:])
            nc.scalar.copy(y_rows[0][:, HALF * h : HALF * (h + 1)], y_half[:])
        for t in range(1, PACK):
            y_psum = psum.tile([P, S], F32, name=f"y_psum{t}", tag=f"bank{t}")
            project(t, 0, S, y_psum[:])
            nc.vector.tensor_copy(y_rows[t][:, :S], y_psum[:])
        half_c = C // 2
        xc_scales = keep.tile([P, C], U8, name="xc_scales", tag="plane", align_bytes=64)
        nc.vector.tensor_copy(xc_scales[:], scales_again[:].indirect(cand_sb[:]))
        xc_words = [
            keep.tile([P, half_c], U32, name="xc_words0", tag="stage1", align_bytes=64),
        ]
        nc.vector.tensor_copy(xc_words[0][:], words[:].indirect(cand_sb[:, : half_c // LANES]))

        z_codes = keep.tile([P, S], U32, name="z_codes", align_bytes=64)
        z_scales = keep.tile([P, S], U8, name="z_scales", align_bytes=64)
        y_n1 = keep.tile([P, PACK, S], F32, name="y_n1")
        y_n2 = keep.tile([P, PACK, S], F32, name="y_n2")
        least = keep.tile([P, PACK - 1, S], F32, name="least")
        diff = keep.tile([P, 2, PACK - 1, HALF], F32, name="diff")
        z_bf = [keep.tile([P, HALF, PACK], BF16, name=f"z_bf{h}", tag=f"z_stage{h}", align_bytes=64) for h in range(2)]
        first, second, every = slice(0, HALF), slice(HALF, S), slice(0, S)

        def fetch(t, cols):
            entries = slice(cols.start // LANES, cols.stop // LANES)
            nc.scalar.activation(y_n1[:, t, cols], y_rows[t][:].indirect(n1_sb[:, entries]), COPY)
            nc.scalar.activation(y_n2[:, t, cols], y_rows[t][:].indirect(n2_sb[:, entries]), COPY)

        def smaller(t, cols, into):
            nc.vector.tensor_tensor(into, y_n1[:, t, cols], y_n2[:, t, cols], ALU.min)

        def differ(t, cols):
            h = cols.start // HALF
            into = diff[:, :, t, :] if cols is every else diff[:, h, t, :]
            rows = y_rows[t][:, cols]
            smallest = least[:, t, cols]
            if cols is every:
                rows = rows.rearrange("p (h s) -> p h s", h=2)
                smallest = smallest.rearrange("p (h s) -> p h s", h=2)
            nc.vector.tensor_tensor(into, rows, smallest, ALU.subtract)

        def last_plane(h, smallest):
            nc.vector.scalar_tensor_tensor(
                z_bf[h][:, :, 3], smallest, minus_gain[:], weighted[:, HALF * h : HALF * (h + 1)], ALU.mult, ALU.add
            )

        def weigh(h, planes):
            nc.vector.tensor_tensor(
                z_bf[h][:, :, :planes].rearrange("p (s i) t -> p s t i", i=2),
                diff[:, h].rearrange("p t (s i) -> p s t i", i=2),
                gain[:, :planes].unsqueeze(1).unsqueeze(3).to_broadcast([P, HALF // 2, planes, 2]),
                ALU.mult,
            )

        def quantize_z(h):
            cols = slice(HALF * h, HALF * (h + 1))
            nc.vector.quantize_mx(
                out=z_codes[:, cols].bitcast(FP8X4),
                scales=z_scales[:, cols],
                in_=z_bf[h][:].rearrange("p s t -> p (s t)"),
            )

        def scores(c, lo, hi, acc):
            rows = slice(P * c, P * (c + 1))
            nc.tensor.matmul_mx(
                out=acc,
                lhsT=xc_words[c // 2][:, P * (c % 2) : P * (c % 2 + 1)].bitcast(FP8X4),
                lhsT_scale=xc_scales[:, rows],
                rhs=z_codes[:, lo:hi].bitcast(FP8X4),
                rhs_scale=z_scales[:, lo:hi],
                start=True,
                stop=True,
            )

        for t, cols in [(0, every), (1, every), (2, first), (2, second), (3, first), (3, second)]:
            fetch(t, cols)

        weighted = keep.tile([P, S], F32, name="weighted")
        minus_gain = keep.tile([P, 1], F32, name="minus_gain")
        nc.vector.tensor_scalar(minus_gain[:], gain[:, 3:4], -1.0, None, ALU.mult)
        nc.vector.tensor_scalar(weighted[:], y_rows[3][:], gain[:, 3:4], None, ALU.mult)
        for t in range(2):
            smaller(t, every, least[:, t, :])
            differ(t, every)
        smaller(2, first, least[:, 2, first])
        differ(2, first)
        smaller(2, second, least[:, 2, second])
        weigh(0, PACK - 1)
        differ(2, second)
        smaller(3, first, least[:, 2, second])
        weigh(1, PACK - 1)
        last_plane(0, least[:, 2, second])
        smaller(3, second, diff[:, 1, 2, :])
        quantize_z(0)
        last_plane(1, diff[:, 1, 2, :])
        quantize_z(1)
        xc_words.append(keep.tile([P, half_c], U32, name="xc_words1", tag="z_stage1", align_bytes=64))
        nc.vector.tensor_copy(xc_words[1][:], words[:].indirect(cand_sb[:, half_c // LANES :]))

        s_halves = [psum.tile([P, HALF], F32, name=f"s_half{h}") for h in range(2)]
        for h, cols in enumerate((first, second)):
            scores(0, cols.start, cols.stop, s_halves[h][:])
            nc.scalar.activation(s_rows[0][:, cols], s_halves[h][:], COPY, scale=0.0625)
        for c in range(1, C // P):
            s_psum = psum.tile([P, S], F32, name=f"s_psum{c}", tag=f"bank{c}")
            scores(c, 0, S, s_psum[:])
            nc.vector.tensor_scalar(s_rows[c][:, :S], s_psum[:], 0.0625, None, ALU.mult)

        def finish(c, cols, largest, smallest, result):
            nc.vector.scalar_tensor_tensor(result[:, cols], smallest[:], -0.5, largest[:], ALU.mult, ALU.add)
            nc.sync.dma_start(out[P * c : P * (c + 1), cols], result[:, cols])

        pending = None
        for c in range(C // P):
            result = keep.tile([P, S], F32, name=f"result{c}")
            last = c == C // P - 1
            if last:
                stretches = [[0, 512], [512, 768], [768, 896], [896, 1024]]
            else:
                stretches = [[[0, 256, 512, 1024]], [[0, 512, 1024]], [[0, 512], [512, 1024]]][c]
            for bounds in stretches:
                base, groups = bounds[0], (bounds[-1] - bounds[0]) // MEMBERS
                largest = ring.tile([P, groups], F32, name="largest")
                smallest = ring.tile([P, groups], F32, name="smallest")
                by_reduce = groups == 32
                if not by_reduce:
                    upper = ring.tile([P, groups, 2], F32, name="upper")
                    lower = ring.tile([P, groups, 2], F32, name="lower")
                for lo, hi in zip(bounds[:-1], bounds[1:]):
                    members = ring.tile([P, hi - lo], F32, name="members")
                    nc.scalar.activation(members[:], s_rows[c][:].indirect(n3_sb[:, lo // LANES : hi // LANES]), COPY)
                    if by_reduce:
                        quads = members[:].rearrange("p (j u) -> p j u", u=MEMBERS)
                        nc.vector.tensor_reduce(largest[:], quads, mybir.AxisListType.X, ALU.max)
                    else:
                        pairs = members[:].rearrange("p (j u v) -> p j u v", u=2, v=2)
                        js = slice((lo - base) // MEMBERS, (hi - base) // MEMBERS)
                        nc.vector.tensor_tensor(upper[:, js, :], pairs[:, :, 0, :], pairs[:, :, 1, :], ALU.max)
                    if pending is not None:
                        finish(*pending)
                        pending = None
                    if by_reduce:
                        nc.vector.tensor_reduce(smallest[:], quads, mybir.AxisListType.X, ALU.min)
                    else:
                        nc.vector.tensor_tensor(lower[:, js, :], pairs[:, :, 0, :], pairs[:, :, 1, :], ALU.min)
                if not by_reduce:
                    nc.vector.tensor_tensor(largest[:], upper[:, :, 0], upper[:, :, 1], ALU.max)
                    nc.vector.tensor_tensor(smallest[:], lower[:, :, 0], lower[:, :, 1], ALU.min)
                pending = (c, slice(base // MEMBERS, base // MEMBERS + groups), largest, smallest, result)
        finish(*pending)
